import numpy as np
import ml_dtypes


def mxq(x, axis, fmt="e4m3"):
    dtype, down = {"e4m3": (ml_dtypes.float8_e4m3fn, 7), "e5m2": (ml_dtypes.float8_e5m2, 14)}[fmt]
    v = np.moveaxis(np.asarray(x, np.float32).astype(ml_dtypes.bfloat16).astype(np.float64), axis, -1)
    blocks = v.reshape(v.shape[:-1] + (-1, 32))
    amax = np.abs(blocks).max(-1, keepdims=True)
    byte = np.maximum(np.where(amax > 0, np.frexp(amax)[1] - 1 + 127, 0) - down, 1)
    scale = np.exp2(byte - 127.0)
    codes = (blocks / scale).astype(np.float32).astype(dtype).astype(np.float64)
    return np.moveaxis((codes * scale).reshape(v.shape), -1, axis)


WIDE = False


def mx_kscale(k):
    if not WIDE:
        return np.ones(k)
    levels = np.array([10, -10, 5, -5, 0])
    if k % 512:
        return np.exp2(np.random.permutation(np.resize(levels, k // 32))).repeat(32)
    a = np.empty((k // 512, 16))
    for p in range(k // 512):
        a[p, :8] = np.random.permutation(np.resize(levels, 8))
        for g in range(8):
            far = levels[np.abs(levels - a[p, g]) >= 10]
            a[p, g + 8] = far[np.random.randint(len(far))]
    return np.exp2(a.ravel()).repeat(32)


def f64(x):
    return np.asarray(x).astype(np.float64)


def striped(idx):
    return np.tile(idx.reshape(-1, 16).T, (8, 1)).astype(np.uint16)


def unstriped(offs):
    return offs[:16].T.reshape(-1).astype(np.int64)


E2M1 = np.array([0.0, 0.5, 1.0, 1.5, 2.0, 3.0, 4.0, 6.0, -0.0, -0.5, -1.0, -1.5, -2.0, -3.0, -4.0, -6.0])


def pack_weight(w, fmt):
    k, n = w.shape
    w = f64(np.asarray(w, np.float32).astype(ml_dtypes.bfloat16)).reshape(k // 32, 32, n)
    amax = np.abs(w).max(1)
    if fmt == "e4m3":
        byte = np.frexp(amax)[1] - 1 + 127 - 7
    else:
        mant, ex = np.frexp(amax / 6.0)
        byte = np.where(mant > 0.5, ex, ex - 1) + 127
    byte = np.clip(np.where(amax > 0, byte, 1), 1, 254)
    scaled = (w * np.exp2(127.0 - byte)[:, None, :]).reshape(k, n).astype(np.float32)
    by_word = np.ascontiguousarray(scaled.reshape(k // 512, 128, 4, n).transpose(0, 1, 3, 2))
    if fmt == "e4m3":
        words = by_word.astype(ml_dtypes.float8_e4m3fn).view(np.uint8)
    else:
        c = by_word.astype(ml_dtypes.float4_e2m1fn).view(np.uint8) & 0xF
        words = (c[..., 0::2] | (c[..., 1::2] << 4)).reshape(k // 512, 128, 2 * n)
    return np.ascontiguousarray(words), np.ascontiguousarray(byte.astype(np.uint8).reshape(k // 512, 16, n))


def unpack_weight(words, scales, fmt):
    g, _, n = scales.shape
    words = np.ascontiguousarray(words).reshape(g, 128, n, -1)
    if fmt == "e4m3":
        vals = words.view(ml_dtypes.float8_e4m3fn).astype(np.float64)
    else:
        nib = np.empty((g, 128, n, 4), np.uint8)
        nib[..., 0::2] = words & 0xF
        nib[..., 1::2] = words >> 4
        vals = E2M1[nib]
    vals = vals * np.repeat(np.exp2(scales.astype(np.float64) - 127.0), 8, axis=1)[..., None]
    return vals.transpose(0, 1, 3, 2).reshape(g * 512, n)


K, T, E, C, N = 2560, 640, 20, 128, 128
TOP = 4


def by_expert(wq, xq):
    return np.concatenate([wq[e].T @ xq[:, e * C:(e + 1) * C] for e in range(E)], axis=1)


def setup_inputs():
    n = np.random.standard_normal
    s = mx_kscale(K)[:, None]
    deal = np.repeat(np.arange(E), C).reshape(TOP, T)[:, np.random.permutation(T)]
    deal = np.take_along_axis(deal, np.argsort(np.random.rand(TOP, T), axis=0), axis=0)
    for _ in range(8):
        s_, t_ = np.random.permutation(T).reshape(2, -1); r = np.random.randint(TOP, size=T // 2); x, y = deal[r, s_].copy(), deal[r, t_].copy()
        ok = ~((deal[:, s_] == y).any(0) | (deal[:, t_] == x).any(0)); deal[r[ok], s_[ok]] = y[ok]; deal[r[ok], t_[ok]] = x[ok]
    order = np.lexsort((np.random.rand(TOP * T), deal.reshape(-1)))
    slot_token = order % T; pos = np.empty(TOP * T, np.int64); pos[order] = np.arange(TOP * T); pos = pos.reshape(TOP, T)
    g = np.random.uniform(0.5, 1.5, (TOP, T)); g = g / g.sum(0)
    x = pack_weight(n((K, T)) * s, "e4m3")
    return {
        "x_words": x[0],
        "x_scales": x[1],
        "w": (n((E, K, N)) / np.sqrt(K) / s[None]).astype(np.float32),
        "gate": np.stack([np.tile(r, (N, 1)) for r in g]).astype(np.float32),
        "offs": striped(slot_token),
        "pos1": striped(pos[0]),
        "pos2": striped(pos[1]),
        "pos3": striped(pos[2]),
        "pos4": striped(pos[3]),
    }


def reference(x_words, x_scales, w, gate, offs, pos1, pos2, pos3, pos4):
    idx = unstriped(offs)
    xq = unpack_weight(x_words, x_scales, "e4m3")[:, idx]
    y = by_expert(mxq(f64(w), 1, "e4m3"), xq)
    return sum(f64(gate[r]) * y[:, unstriped(p)] for r, p in enumerate((pos1, pos2, pos3, pos4)))

from contextlib import ExitStack

import concourse.mybir as mybir

K, T, E, C, N = 2560, 640, 20, 128, 128
TOP = 4
SLOTS = E * C
FLOPS = 2 * K * N * SLOTS

F32 = mybir.dt.float32
BF16 = mybir.dt.bfloat16
I32 = mybir.dt.int32
U32 = mybir.dt.uint32
U16 = mybir.dt.uint16
U8 = mybir.dt.uint8
FP8X4 = mybir.dt.float8_e4m3fn_x4
MULT = mybir.AluOpType.mult
ADD = mybir.AluOpType.add

P = 128
PACK = 4
K_PASS = P * PACK
PASSES = K // K_PASS
PACKED_PLANES = 4
GROUP = 4
GROUP_SLOTS = GROUP * C
WINDOW = 704
HALF = T // 2


def tile_moe_pkd_lin_none_kernel(
    tc, x_words, x_scales, w, gate, offs, pos1, pos2, pos3, pos4, out
):
    nc = tc.nc
    with ExitStack() as ctx:
        keep = ctx.enter_context(tc.tile_pool(name="keep", bufs=1))
        stream = ctx.enter_context(tc.tile_pool(name="stream", bufs=24))
        rounded = ctx.enter_context(tc.tile_pool(name="rounded", bufs=48))
        coded = ctx.enter_context(tc.tile_pool(name="coded", bufs=10))
        slots = ctx.enter_context(tc.tile_pool(name="slots", bufs=3))
        psum = ctx.enter_context(tc.psum_pool(name="psum", bufs=1))

        slot_list = keep.tile([P, SLOTS // 16], U16, name="slot_list")
        nc.sync.dma_start(slot_list[:], offs)

        token_words = []
        for o in range(PASSES):
            words = keep.tile([P, WINDOW], I32, name="token_words%d" % o, align_bytes=64)
            nc.vector.memset(words[:, T:WINDOW], 0)
            nc.sync.dma_start(words[:, 0:T], x_words[o].rearrange("p t r -> p (t r)").bitcast(I32))
            token_words.append(words)

        token_scales = keep.tile([P, WINDOW], U8, name="token_scales", align_bytes=64)
        slot_scales = keep.tile([P, SLOTS], U8, name="slot_scales", align_bytes=64)
        last_scales = keep.tile([P, SLOTS], U8, name="last_scales", align_bytes=64)
        nc.gpsimd.memset(token_scales[:].bitcast(I32), 0)
        for q in range(4):
            nc.gpsimd.dma_start(
                token_scales[32 * q : 32 * q + 4 * PASSES, 0:T].bitcast(I32),
                x_scales[:, 4 * q : 4 * q + 4, :].bitcast(I32),
            )
        nc.gpsimd.memset(last_scales[:].bitcast(I32), 0)
        for g in range(E // GROUP):
            entries = slot_list[:, g * GROUP_SLOTS // 16 : (g + 1) * GROUP_SLOTS // 16]
            nc.vector.tensor_copy(
                slot_scales[:, g * GROUP_SLOTS : (g + 1) * GROUP_SLOTS], token_scales[:].indirect(entries)
            )
        for i in range(4):
            nc.gpsimd.dma_start(
                last_scales[i:P:32, :].bitcast(I32), slot_scales[4 * PACKED_PLANES + i : P : 32, :].bitcast(I32)
            )

        y = keep.tile([P, SLOTS], F32, name="y")

        for g in range(E // GROUP):
            entries = slot_list[:, g * GROUP_SLOTS // 16 : (g + 1) * GROUP_SLOTS // 16]
            slot_words = []
            for o in range(PASSES):
                gathered = slots.tile([P, GROUP_SLOTS], U32, name="slot_words%d" % o, align_bytes=64)
                nc.vector.tensor_copy(gathered[:], token_words[o][:].bitcast(U32).indirect(entries))
                slot_words.append(gathered)

            bank = psum.tile([P, GROUP_SLOTS], F32, name="bank%d" % g)
            for c in range(GROUP):
                e = g * GROUP + c
                cols = slice(c * C, (c + 1) * C)
                last = e == E - 1
                if last:
                    last_bank = psum.tile([P, C], F32, name="last_bank")
                    acc = last_bank[:]
                else:
                    acc = bank[:, cols]
                for o in range(PASSES):
                    raw = stream.tile([P, PACK, N], F32, name="raw", tag="stream")
                    nc.sync.dma_start(
                        raw[:], w[e, o * K_PASS : (o + 1) * K_PASS, :].rearrange("(p t) n -> p t n", t=PACK)
                    )
                    woven = rounded.tile([P, N * PACK], BF16, name="woven", align_bytes=64)
                    nc.scalar.copy(
                        woven[:].rearrange("p (c i t) -> p c t i", i=4, t=PACK),
                        raw[:].rearrange("p t (c i) -> p c t i", i=4),
                    )
                    codes = coded.tile([P, N], U32, name="codes", align_bytes=64)
                    w_scales = coded.tile([P, N], U8, name="w_scales", align_bytes=64)
                    nc.vector.quantize_mx(out=codes[:].bitcast(FP8X4), scales=w_scales[:], in_=woven[:])
                    if o < PACKED_PLANES:
                        x_plane = slot_scales[4 * o : P, e * C : (e + 1) * C]
                    else:
                        x_plane = last_scales[:, e * C : (e + 1) * C]
                    nc.tensor.matmul_mx(
                        out=acc,
                        lhsT=codes[:].bitcast(FP8X4),
                        lhsT_scale=w_scales[:],
                        rhs=slot_words[o][:, cols].bitcast(FP8X4),
                        rhs_scale=x_plane,
                        start=(o == 0),
                        stop=(o == PASSES - 1),
                    )
                if e == E - 2:
                    nc.vector.tensor_copy(y[:, g * GROUP_SLOTS : (e + 1) * C], bank[:, 0 : (c + 1) * C])
                elif last:
                    nc.vector.tensor_copy(y[:, e * C : (e + 1) * C], acc)
                elif c == GROUP - 1:
                    nc.vector.tensor_copy(y[:, g * GROUP_SLOTS : (g + 1) * GROUP_SLOTS], bank[:])

        gates = []
        places = []
        for r, pos in enumerate((pos1, pos2, pos3, pos4)):
            gate_r = stream.tile([P, T], F32, name="gate_r", tag="stream")
            nc.sync.dma_start(gate_r[:], gate[r])
            gates.append(gate_r)
            place = keep.tile([P, T // 16], U16, name="place%d" % r)
            nc.sync.dma_start(place[:], pos)
            places.append(place)

        for h in range(2):
            tokens = slice(h * HALF, (h + 1) * HALF)
            terms = keep.tile([P, TOP, HALF], F32, name="terms%d" % h)
            for r in range(TOP):
                nc.vector.tensor_tensor(
                    terms[:, r, :],
                    y[:].indirect(places[r][:, h * HALF // 16 : (h + 1) * HALF // 16]),
                    gates[r][:, tokens],
                    MULT,
                )
            pairs = keep.tile([P, 2, HALF], F32, name="pairs%d" % h)
            nc.vector.tensor_tensor(pairs[:], terms[:, 0:2, :], terms[:, 2:4, :], ADD)
            total = keep.tile([P, HALF], F32, name="total%d" % h)
            nc.vector.tensor_tensor(total[:], pairs[:, 0, :], pairs[:, 1, :], ADD)
            nc.sync.dma_start(out[:, tokens], total[:])
